import numpy as np
import ml_dtypes


def mxq(x, axis, fmt="e4m3"):
    dtype, down = {"e4m3": (ml_dtypes.float8_e4m3fn, 7), "e5m2": (ml_dtypes.float8_e5m2, 14)}[fmt]
    v = np.moveaxis(np.asarray(x, np.float32).astype(ml_dtypes.bfloat16).astype(np.float64), axis, -1)
    blocks = v.reshape(v.shape[:-1] + (-1, 32))
    amax = np.abs(blocks).max(-1, keepdims=True)
    byte = np.maximum(np.where(amax > 0, np.frexp(amax)[1] - 1 + 127, 0) - down, 1)
    scale = np.exp2(byte - 127.0)
    codes = (blocks / scale).astype(np.float32).astype(dtype).astype(np.float64)
    return np.moveaxis((codes * scale).reshape(v.shape), -1, axis)


WIDE = False


def mx_kscale(k):
    if not WIDE:
        return np.ones(k)
    levels = np.array([10, -10, 5, -5, 0])
    if k % 512:
        return np.exp2(np.random.permutation(np.resize(levels, k // 32))).repeat(32)
    a = np.empty((k // 512, 16))
    for p in range(k // 512):
        a[p, :8] = np.random.permutation(np.resize(levels, 8))
        for g in range(8):
            far = levels[np.abs(levels - a[p, g]) >= 10]
            a[p, g + 8] = far[np.random.randint(len(far))]
    return np.exp2(a.ravel()).repeat(32)


def f64(x):
    return np.asarray(x).astype(np.float64)


def striped8(idx):
    return np.asarray(idx).reshape(8, -1, 16).transpose(0, 2, 1).reshape(128, -1).astype(np.uint16)


def unstriped8(offs):
    return offs.reshape(8, 16, -1).transpose(0, 2, 1).reshape(8, -1).astype(np.int64)


def pick8(x, idx, run):
    r = np.arange(len(x))
    return x[r[:, None], idx[r % (8 * run) // run]]


E2M1 = np.array([0.0, 0.5, 1.0, 1.5, 2.0, 3.0, 4.0, 6.0, -0.0, -0.5, -1.0, -1.5, -2.0, -3.0, -4.0, -6.0])


def pack_weight(w, fmt):
    k, n = w.shape
    w = f64(np.asarray(w, np.float32).astype(ml_dtypes.bfloat16)).reshape(k // 32, 32, n)
    amax = np.abs(w).max(1)
    if fmt == "e4m3":
        byte = np.frexp(amax)[1] - 1 + 127 - 7
    else:
        mant, ex = np.frexp(amax / 6.0)
        byte = np.where(mant > 0.5, ex, ex - 1) + 127
    byte = np.clip(np.where(amax > 0, byte, 1), 1, 254)
    scaled = (w * np.exp2(127.0 - byte)[:, None, :]).reshape(k, n).astype(np.float32)
    by_word = np.ascontiguousarray(scaled.reshape(k // 512, 128, 4, n).transpose(0, 1, 3, 2))
    if fmt == "e4m3":
        words = by_word.astype(ml_dtypes.float8_e4m3fn).view(np.uint8)
    else:
        c = by_word.astype(ml_dtypes.float4_e2m1fn).view(np.uint8) & 0xF
        words = (c[..., 0::2] | (c[..., 1::2] << 4)).reshape(k // 512, 128, 2 * n)
    return np.ascontiguousarray(words), np.ascontiguousarray(byte.astype(np.uint8).reshape(k // 512, 16, n))


def unpack_weight(words, scales, fmt):
    g, _, n = scales.shape
    words = np.ascontiguousarray(words).reshape(g, 128, n, -1)
    if fmt == "e4m3":
        vals = words.view(ml_dtypes.float8_e4m3fn).astype(np.float64)
    else:
        nib = np.empty((g, 128, n, 4), np.uint8)
        nib[..., 0::2] = words & 0xF
        nib[..., 1::2] = words >> 4
        vals = E2M1[nib]
    vals = vals * np.repeat(np.exp2(scales.astype(np.float64) - 127.0), 8, axis=1)[..., None]
    return vals.transpose(0, 1, 3, 2).reshape(g * 512, n)


D, E, T, Q, I = 512, 512, 1024, 128, 512


def setup_inputs():
    n = np.random.standard_normal
    idx = np.stack([np.random.permutation(T)[:I] for _ in range(8)])
    idx2 = np.stack([np.random.permutation(T)[:I] for _ in range(8)])
    fd = mx_kscale(D)
    fe = mx_kscale(E)
    keysp = pack_weight(n((D, T)) / fd[:, None], "e2m1")
    return {
        "query": (n((D, Q)) * 0.6 / np.sqrt(D) * fd[:, None]).astype(np.float32),
        "keys_words": keysp[0],
        "keys_scales": keysp[1],
        "gout": (n((E, Q)) * 1 / np.sqrt(E) * fe[:, None]).astype(np.float32),
        "vals": (n((E, T)) / fe[:, None]).astype(np.float32),
        "share": (np.random.uniform(0.4, 0.9, (Q, 1))).astype(np.float32),
        "fac": (np.random.uniform(0.5, 2.0, (1, T))).astype(np.float32),
        "dquery": (n((D, Q)) * 1.0 / np.sqrt(D) * fd[:, None]).astype(np.float32),
        "base": (0.5 * n((Q, T))).astype(np.float32),
        "offs": striped8(idx),
        "offs2": striped8(idx2),
    }


def reference(query, keys_words, keys_scales, gout, vals, share, fac, dquery, base, offs, offs2):
    idx = unstriped8(offs)
    idx2 = unstriped8(offs2)
    keysu = unpack_weight(keys_words, keys_scales, "e2m1")
    queryq = mxq(f64(query), 0, "e4m3")
    a = queryq.T @ keysu
    dqueryq = mxq(f64(dquery), 0, "e4m3")
    ta = dqueryq.T @ keysu
    dl = (pick8(a, idx2, 16) - pick8(a, idx, 16)) * f64(share)
    df0 = np.zeros((Q, T))
    df0[np.arange(Q)[:, None], idx[np.arange(Q) % 128 // 16]] = dl
    s = a + df0
    p = np.exp(s - np.max(s, axis=1, keepdims=True))
    z = np.sum(p, axis=1, keepdims=True)
    goutq = mxq(f64(gout), 0, "e4m3")
    valsq = mxq(f64(vals), 0, "e4m3")
    c0 = goutq.T @ valsq
    dz = np.sum(c0 * p * f64(fac) / np.square(z) * (-1.0), axis=1, keepdims=True)
    dp = c0 / z * f64(fac) + dz
    xdl = (pick8(ta, idx2, 16) - pick8(ta, idx, 16)) * f64(share)
    xdf0 = np.zeros((Q, T))
    xdf0[np.arange(Q)[:, None], idx[np.arange(Q) % 128 // 16]] = xdl
    xs = ta + xdf0
    xp = xs * p
    xz = np.sum(xp, axis=1, keepdims=True)
    xdz = np.sum((xp * f64(fac) * c0 - xz * z * 2.0 * c0 * p * f64(fac) / np.square(z)) / np.square(z) * (-1.0), axis=1, keepdims=True)
    xdp = xz * c0 / np.square(z) * (-1.0) * f64(fac) + xdz
    xds = xdp * p + xp * dp
    xddl = pick8(xds, idx, 16)
    xe1 = xddl * f64(share)
    xs1 = np.zeros((Q, T))
    xs1[np.arange(Q)[:, None], idx2[np.arange(Q) % 128 // 16]] = xe1
    xe2 = xddl * f64(share) * (-1.0)
    xs2 = np.zeros((Q, T))
    xs2[np.arange(Q)[:, None], idx[np.arange(Q) % 128 // 16]] = xe2
    xda = xds + xs1 + xs2
    y = xda * 1024.0 + f64(base)
    return y

@@ -1,0 +1,285 @@
+from contextlib import ExitStack
+
+import concourse.mybir as mybir
+from concourse.masks import make_identity
+
+D, E, T, Q, I = 512, 512, 1024, 128, 512
+FLOPS = 2 * Q * T * (2 * D + E)
+
+F32 = mybir.dt.float32
+BF16 = mybir.dt.bfloat16
+I32 = mybir.dt.int32
+U32 = mybir.dt.uint32
+U16 = mybir.dt.uint16
+U8 = mybir.dt.uint8
+FP8X4 = mybir.dt.float8_e4m3fn_x4
+FP4X4 = mybir.dt.float4_e2m1fn_x4
+ALU = mybir.AluOpType
+ACT = mybir.ActivationFunctionType
+
+P = 128
+PACK = 4
+BANK = 512
+HALVES = T // BANK
+BLOCKS = T // P
+PER_BANK = BANK // P
+QUARTER = 256
+OUT_FACTOR = 1024.0
+
+
+def interleave(copy, grouped, raw):
+    copy(
+        out=grouped.rearrange("p (c i t) -> p c t i", i=4, t=PACK),
+        in_=raw.rearrange("p t (c i) -> p c t i", i=4),
+    )
+
+
+def tile_attend_hvborrowed_heads_kernel(
+    tc, query, keys_words, keys_scales, gout, vals, share, fac, dquery, base, offs, offs2, out
+):
+    nc = tc.nc
+    with ExitStack() as ctx:
+        lists = ctx.enter_context(tc.tile_pool(name="lists", bufs=1))
+        sb = ctx.enter_context(tc.tile_pool(name="sb", bufs=1))
+        ps = ctx.enter_context(tc.psum_pool(name="ps", bufs=1))
+
+        def half(h):
+            return slice(h * BANK, (h + 1) * BANK)
+
+        def block(b):
+            return slice(b * P, (b + 1) * P)
+
+        def banks(tag):
+            return [ps.tile([P, BANK], F32, name="%s%d" % (tag, h), tag="%s%d" % (tag, h)) for h in range(HALVES)]
+
+        def bank_block(pair, b):
+            return pair[b // PER_BANK][:, block(b % PER_BANK)]
+
+        k_scales = sb.tile([P, T], U8, align_bytes=64)
+        nc.vector.memset(k_scales[:].bitcast(U32), 0)
+
+        q_raw = sb.tile([P, PACK, Q], F32)
+        nc.sync.dma_start(out=q_raw[:], in_=query.rearrange("(p t) w -> p t w", t=PACK))
+        k_words = sb.tile([P, 2 * T], U8, align_bytes=64)
+        nc.sync.dma_start(out=k_words[:].bitcast(I32), in_=keys_words[0].bitcast(I32))
+        for quad in range(4):
+            nc.sync.dma_start(
+                out=k_scales[32 * quad : 32 * quad + 4, :].bitcast(I32),
+                in_=keys_scales[0, 4 * quad : 4 * quad + 4, :].bitcast(I32),
+            )
+        dq_raw = sb.tile([P, PACK, Q], F32)
+        nc.sync.dma_start(out=dq_raw[:], in_=dquery.rearrange("(p t) w -> p t w", t=PACK))
+        list1 = lists.tile([P, I // 16], U16)
+        nc.sync.dma_start(list1[:], offs)
+        list2 = lists.tile([P, I // 16], U16)
+        nc.sync.dma_start(list2[:], offs2)
+        share_col = sb.tile([P, 1], F32)
+        nc.sync.dma_start(out=share_col[:], in_=share)
+        g_raw = sb.tile([P, PACK, Q], F32)
+        nc.sync.dma_start(out=g_raw[:], in_=gout.rearrange("(p t) w -> p t w", t=PACK))
+        v_raw = []
+        for c in range(T // QUARTER):
+            chunk = sb.tile([P, PACK, QUARTER], F32, name="v_raw%d" % c, tag="v_raw%d" % c)
+            nc.sync.dma_start(
+                out=chunk[:],
+                in_=vals[:, c * QUARTER : (c + 1) * QUARTER].rearrange("(p t) w -> p t w", t=PACK),
+            )
+            v_raw.append(chunk)
+        fac_rows = sb.tile([P, P], F32)
+        nc.gpsimd.memset(fac_rows[:], 0.0)
+        nc.sync.dma_start(out=fac_rows[0:BLOCKS, :], in_=fac.rearrange("o (c p) -> (o c) p", p=P))
+        base_sb = sb.tile([P, T], F32)
+        nc.sync.dma_start(out=base_sb[:], in_=base)
+
+        ident = sb.tile([P, P], F32)
+        make_identity(nc, ident[:])
+
+        placed1 = sb.tile([P, T], F32)
+        placed2 = sb.tile([P, T], F32)
+        nc.vector.memset(placed1[:], 0.0)
+        nc.vector.memset(placed2[:], 0.0)
+
+        def quantised(name, copy, raw):
+            grouped = sb.tile([P, PACK * Q], BF16, align_bytes=64, name=name + "_bf")
+            codes = sb.tile([P, Q], U32, align_bytes=64, name=name + "_codes")
+            scales = sb.tile([P, Q], U8, align_bytes=64, name=name + "_scales")
+            interleave(copy, grouped[:], raw[:])
+            nc.vector.quantize_mx(out=codes[:].bitcast(FP8X4), scales=scales[:], in_=grouped[:])
+            return codes, scales
+
+        def against_keys(acc, codes, scales, col0, width):
+            nc.tensor.matmul_mx(
+                out=acc,
+                lhsT=codes[:].bitcast(FP8X4),
+                lhsT_scale=scales[:],
+                rhs=k_words[:, 2 * col0 : 2 * (col0 + width)].bitcast(FP4X4),
+                rhs_scale=k_scales[:, col0 : col0 + width],
+                start=True,
+                stop=True,
+            )
+
+        def add_turned(acc, src, first, last):
+            for b in range(BLOCKS):
+                nc.tensor.matmul(
+                    out=bank_block(acc, b),
+                    lhsT=src[:, block(b)],
+                    rhs=ident[:],
+                    start=first and b % PER_BANK == 0,
+                    stop=last and b % PER_BANK == PER_BANK - 1,
+                    is_transpose=True,
+                )
+
+        def turn_back(acc_back, staged, acc):
+            for h in range(HALVES):
+                nc.scalar.copy(out=staged[:, half(h)], in_=acc[h][:])
+            for b in range(BLOCKS):
+                nc.tensor.transpose(bank_block(acc_back, b), staged[:, block(b)], ident[:])
+
+        q_codes, q_scales = quantised("q", nc.vector.tensor_copy, q_raw)
+        a_ps = banks("w") + banks("x")
+        a_sb = sb.tile([P, T], F32)
+        for c in range(T // QUARTER):
+            acc = a_ps[c][:, 0:QUARTER]
+            against_keys(acc, q_codes, q_scales, c * QUARTER, QUARTER)
+            copy = (nc.scalar.copy, nc.vector.tensor_copy)[c % 2]
+            copy(out=a_sb[:, c * QUARTER : (c + 1) * QUARTER], in_=acc)
+
+        dq_codes, dq_scales = quantised("dq", nc.vector.tensor_copy, dq_raw)
+        ta_ps = banks("y")
+        ta_sb = sb.tile([P, T], F32)
+        for h in range(HALVES):
+            against_keys(ta_ps[h][:], dq_codes, dq_scales, h * BANK, BANK)
+            nc.scalar.copy(out=ta_sb[:, half(h)], in_=ta_ps[h][:])
+
+        share_wide = sb.tile([P, I], F32)
+        nc.scalar.activation(out=share_wide[:], in_=share_col[:].to_broadcast([P, I]), func=ACT.Copy)
+
+        slot_a = sb.tile([P, I], F32)
+        slot_b = sb.tile([P, I], F32)
+        nc.vector.tensor_copy(out=slot_a[:], in_=a_sb[:].indirect(list1[:]))
+        nc.vector.tensor_tensor(out=slot_b[:], in0=a_sb[:].indirect(list2[:]), in1=slot_a[:], op=ALU.subtract)
+        nc.vector.tensor_tensor(out=placed1[:].indirect(list1[:]), in0=slot_b[:], in1=share_wide[:], op=ALU.mult)
+        nc.vector.tensor_copy(out=slot_b[:], in_=ta_sb[:].indirect(list1[:]))
+
+        g_codes, g_scales = quantised("g", nc.scalar.copy, g_raw)
+        v_codes = sb.tile([P, T], U32, align_bytes=64)
+        v_scales = sb.tile([P, T], U8, align_bytes=64)
+        for h in range(HALVES):
+            v_bf = sb.tile([P, PACK * BANK], BF16, align_bytes=64, name="v_bf%d" % h, tag="v_bf%d" % h)
+            for c in range(BANK // QUARTER):
+                cols = slice(c * PACK * QUARTER, (c + 1) * PACK * QUARTER)
+                interleave(nc.scalar.copy, v_bf[:, cols], v_raw[2 * h + c][:])
+            nc.vector.quantize_mx(
+                out=v_codes[:, half(h)].bitcast(FP8X4), scales=v_scales[:, half(h)], in_=v_bf[:]
+            )
+
+        fac_ps = ps.tile([P, BANK], F32, tag="z0")
+        nc.tensor.transpose(fac_ps[:, 0:P], fac_rows[:], ident[:])
+        fac_cols = sb.tile([P, BLOCKS], F32)
+        nc.scalar.activation(out=fac_cols[:], in_=fac_ps[:, 0:BLOCKS], func=ACT.Copy, scale=-OUT_FACTOR)
+
+        s_turned = banks("w")
+        add_turned(s_turned, a_sb, True, False)
+        add_turned(s_turned, placed1, False, True)
+        staged = sb.tile([P, T], F32, tag="v_raw3")
+        s_ps = banks("x")
+        turn_back(s_ps, staged, s_turned)
+
+        xdiff = sb.tile([P, I], F32, align_bytes=64, tag="v_bf1")
+        nc.vector.tensor_tensor(out=xdiff[:], in0=ta_sb[:].indirect(list2[:]), in1=slot_b[:], op=ALU.subtract)
+        nc.vector.tensor_tensor(out=placed1[:].indirect(list1[:]), in0=xdiff[:], in1=share_wide[:], op=ALU.mult)
+
+        xs = sb.tile([P, T], F32)
+        neg_s = sb.tile([P, T], F32)
+        neg_max = sb.tile([P, 1], F32)
+        nc.vector.tensor_scalar(
+            out=neg_s[:, half(0)], in0=s_ps[0][:], scalar1=-1.0, scalar2=None,
+            op0=ALU.mult, op1=ALU.min, accum_out=xs[:, 0:1],
+        )
+        nc.vector.tensor_scalar(
+            out=neg_s[:, half(1)], in0=s_ps[1][:], scalar1=-1.0, scalar2=xs[:, 0:1],
+            op0=ALU.mult, op1=ALU.min, accum_out=neg_max[:],
+        )
+
+        c0_turned = banks("w")
+        cf_turned = sb.tile([P, T], F32)
+        cf_ps = banks("y")
+        for b in range(BLOCKS):
+            nc.tensor.matmul_mx(
+                out=bank_block(c0_turned, b),
+                lhsT=v_codes[:, block(b)].bitcast(FP8X4),
+                lhsT_scale=v_scales[:, block(b)],
+                rhs=g_codes[:].bitcast(FP8X4),
+                rhs_scale=g_scales[:],
+                start=True,
+                stop=True,
+            )
+        for b in range(BLOCKS):
+            nc.scalar.activation(
+                out=cf_turned[:, block(b)], in_=bank_block(c0_turned, b), func=ACT.Copy,
+                scale=fac_cols[:, b : b + 1],
+            )
+        for b in range(BLOCKS):
+            nc.tensor.transpose(bank_block(cf_ps, b), cf_turned[:, block(b)], ident[:])
+
+        p = sb.tile([P, T], F32)
+        z = sb.tile([P, 1], F32)
+        nc.scalar.activation(out=p[:], in_=neg_s[:], func=ACT.Exp, bias=neg_max[:], scale=-1.0, accum_out=z[:])
+
+        nc.vector.tensor_tensor(out=xs[:], in0=ta_sb[:], in1=placed1[:], op=ALU.add)
+        inv_z = sb.tile([P, 1], F32)
+        nc.vector.reciprocal(out=inv_z[:], in_=z[:])
+        prob = sb.tile([P, T], F32)
+        nc.scalar.activation(out=prob[:], in_=p[:], func=ACT.Copy, scale=inv_z[:])
+
+
+        neg_share_wide = sb.tile([P, I], F32)
+        nc.scalar.activation(out=neg_share_wide[:], in_=share_wide[:], func=ACT.Copy, scale=-1.0)
+        y_turned = banks("z")
+        add_turned(y_turned, base_sb, True, False)
+
+        sums = sb.tile([P, 8], F32)
+        spent = sb.tile([P, T], F32)
+        pw = sb.tile([P, T], F32)
+        t1 = sb.tile([P, T], F32)
+        xds = sb.tile([P, T], F32)
+        for h in range(HALVES):
+            nc.vector.scalar_tensor_tensor(
+                out=spent[:, half(h)], in0=cf_ps[h][:], scalar=1.0, in1=p[:, half(h)],
+                op0=ALU.mult, op1=ALU.mult, accum_out=sums[:, h : h + 1],
+            )
+        nc.vector.tensor_scalar(
+            out=sums[:, 2:3], in0=sums[:, 0:1], scalar1=sums[:, 1:2], scalar2=inv_z[:],
+            op0=ALU.add, op1=ALU.mult,
+        )
+        nc.vector.scalar_tensor_tensor(
+            out=spent[:], in0=xs[:], scalar=1.0, in1=prob[:],
+            op0=ALU.mult, op1=ALU.mult, accum_out=sums[:, 3:4],
+        )
+        for h in range(HALVES):
+            nc.vector.scalar_tensor_tensor(
+                out=pw[:, half(h)], in0=cf_ps[h][:], scalar=sums[:, 2:3], in1=prob[:, half(h)],
+                op0=ALU.subtract, op1=ALU.mult,
+            )
+        nc.vector.scalar_tensor_tensor(
+            out=t1[:], in0=xs[:], scalar=sums[:, 3:4], in1=pw[:],
+            op0=ALU.subtract, op1=ALU.mult, accum_out=sums[:, 4:5],
+        )
+        nc.vector.scalar_tensor_tensor(
+            out=xds[:], in0=prob[:], scalar=sums[:, 4:5], in1=t1[:], op0=ALU.mult, op1=ALU.subtract
+        )
+
+        nc.vector.tensor_copy(out=slot_a[:], in_=xds[:].indirect(list1[:]))
+        nc.vector.tensor_tensor(out=placed2[:].indirect(list2[:]), in0=slot_a[:], in1=share_wide[:], op=ALU.mult)
+        nc.vector.tensor_tensor(out=placed1[:].indirect(list1[:]), in0=slot_a[:], in1=neg_share_wide[:], op=ALU.mult)
+
+        add_turned(y_turned, xds, False, False)
+        add_turned(y_turned, placed2, False, True)
+        y_ps = banks("w")
+        turn_back(y_ps, staged, y_turned)
+
+        y = sb.tile([P, T], F32)
+        for c in range(T // QUARTER):
+            cols = slice(c * QUARTER, (c + 1) * QUARTER)
+            nc.vector.tensor_tensor(out=y[:, cols], in0=y_ps[c // 2][:, (c % 2) * QUARTER : (c % 2 + 1) * QUARTER], in1=placed1[:, cols], op=ALU.add)
+            nc.sync.dma_start(out=out[:, cols], in_=y[:, cols])

@@ -49,6 +49,12 @@ def tile_attend_hvborrowed_heads_kernel(
         def block(b):
             return slice(b * P, (b + 1) * P)
 
+        def slots(u):
+            return slice(u * I // 2, (u + 1) * I // 2)
+
+        def entries(u):
+            return slice(u * I // 32, (u + 1) * I // 32)
+
         def banks(tag):
             return [ps.tile([P, BANK], F32, name="%s%d" % (tag, h), tag="%s%d" % (tag, h)) for h in range(HALVES)]
 
@@ -75,8 +81,9 @@ def tile_attend_hvborrowed_heads_kernel(
         nc.sync.dma_start(list2[:], offs2)
         share_col = sb.tile([P, 1], F32)
         nc.sync.dma_start(out=share_col[:], in_=share)
-        g_raw = sb.tile([P, PACK, Q], F32)
-        nc.sync.dma_start(out=g_raw[:], in_=gout.rearrange("(p t) w -> p t w", t=PACK))
+        fac_rows = sb.tile([P, P], F32)
+        nc.gpsimd.memset(fac_rows[:], 0.0)
+        nc.sync.dma_start(out=fac_rows[0:BLOCKS, :], in_=fac.rearrange("o (c p) -> (o c) p", p=P))
         v_raw = []
         for c in range(T // QUARTER):
             chunk = sb.tile([P, PACK, QUARTER], F32, name="v_raw%d" % c, tag="v_raw%d" % c)
@@ -85,9 +92,8 @@ def tile_attend_hvborrowed_heads_kernel(
                 in_=vals[:, c * QUARTER : (c + 1) * QUARTER].rearrange("(p t) w -> p t w", t=PACK),
             )
             v_raw.append(chunk)
-        fac_rows = sb.tile([P, P], F32)
-        nc.gpsimd.memset(fac_rows[:], 0.0)
-        nc.sync.dma_start(out=fac_rows[0:BLOCKS, :], in_=fac.rearrange("o (c p) -> (o c) p", p=P))
+        g_raw = sb.tile([P, PACK, Q], F32)
+        nc.sync.dma_start(out=g_raw[:], in_=gout.rearrange("(p t) w -> p t w", t=PACK))
         base_sb = sb.tile([P, T], F32)
         nc.sync.dma_start(out=base_sb[:], in_=base)
 
@@ -154,14 +160,28 @@ def tile_attend_hvborrowed_heads_kernel(
         share_wide = sb.tile([P, I], F32)
         nc.scalar.activation(out=share_wide[:], in_=share_col[:].to_broadcast([P, I]), func=ACT.Copy)
 
+        fac_ps = ps.tile([P, BANK], F32, tag="z0")
+        nc.tensor.transpose(fac_ps[:, 0:P], fac_rows[:], ident[:])
+        fac_cols = sb.tile([P, BLOCKS], F32)
+        nc.scalar.activation(out=fac_cols[:], in_=fac_ps[:, 0:BLOCKS], func=ACT.Copy, scale=-OUT_FACTOR)
+
         slot_a = sb.tile([P, I], F32)
         slot_b = sb.tile([P, I], F32)
-        nc.vector.tensor_copy(out=slot_a[:], in_=a_sb[:].indirect(list1[:]))
-        nc.vector.tensor_tensor(out=slot_b[:], in0=a_sb[:].indirect(list2[:]), in1=slot_a[:], op=ALU.subtract)
+        for u in range(2):
+            nc.vector.tensor_copy(out=slot_a[:, slots(u)], in_=a_sb[:].indirect(list1[:, entries(u)]))
+        for u in range(2):
+            nc.vector.tensor_tensor(
+                out=slot_b[:, slots(u)], in0=a_sb[:].indirect(list2[:, entries(u)]), in1=slot_a[:, slots(u)],
+                op=ALU.subtract,
+            )
         nc.vector.tensor_tensor(out=placed1[:].indirect(list1[:]), in0=slot_b[:], in1=share_wide[:], op=ALU.mult)
         nc.vector.tensor_copy(out=slot_b[:], in_=ta_sb[:].indirect(list1[:]))
+        xdiff = sb.tile([P, I], F32)
+        nc.vector.tensor_tensor(
+            out=xdiff[:, slots(0)], in0=ta_sb[:].indirect(list2[:, entries(0)]), in1=slot_b[:, slots(0)],
+            op=ALU.subtract,
+        )
 
-        g_codes, g_scales = quantised("g", nc.scalar.copy, g_raw)
         v_codes = sb.tile([P, T], U32, align_bytes=64)
         v_scales = sb.tile([P, T], U8, align_bytes=64)
         for h in range(HALVES):
@@ -173,10 +193,7 @@ def tile_attend_hvborrowed_heads_kernel(
                 out=v_codes[:, half(h)].bitcast(FP8X4), scales=v_scales[:, half(h)], in_=v_bf[:]
             )
 
-        fac_ps = ps.tile([P, BANK], F32, tag="z0")
-        nc.tensor.transpose(fac_ps[:, 0:P], fac_rows[:], ident[:])
-        fac_cols = sb.tile([P, BLOCKS], F32)
-        nc.scalar.activation(out=fac_cols[:], in_=fac_ps[:, 0:BLOCKS], func=ACT.Copy, scale=-OUT_FACTOR)
+        g_codes, g_scales = quantised("g", nc.scalar.copy, g_raw)
 
         s_turned = banks("w")
         add_turned(s_turned, a_sb, True, False)
@@ -185,21 +202,24 @@ def tile_attend_hvborrowed_heads_kernel(
         s_ps = banks("x")
         turn_back(s_ps, staged, s_turned)
 
-        xdiff = sb.tile([P, I], F32, align_bytes=64, tag="v_bf1")
-        nc.vector.tensor_tensor(out=xdiff[:], in0=ta_sb[:].indirect(list2[:]), in1=slot_b[:], op=ALU.subtract)
-        nc.vector.tensor_tensor(out=placed1[:].indirect(list1[:]), in0=xdiff[:], in1=share_wide[:], op=ALU.mult)
 
         xs = sb.tile([P, T], F32)
-        neg_s = sb.tile([P, T], F32)
+        neg_s = sb.tile([P, T], F32, align_bytes=64, tag="v_bf1")
         neg_max = sb.tile([P, 1], F32)
         nc.vector.tensor_scalar(
             out=neg_s[:, half(0)], in0=s_ps[0][:], scalar1=-1.0, scalar2=None,
-            op0=ALU.mult, op1=ALU.min, accum_out=xs[:, 0:1],
+            op0=ALU.mult, op1=ALU.min, accum_out=xdiff[:, I - 1 : I],
         )
         nc.vector.tensor_scalar(
-            out=neg_s[:, half(1)], in0=s_ps[1][:], scalar1=-1.0, scalar2=xs[:, 0:1],
+            out=neg_s[:, half(1)], in0=s_ps[1][:], scalar1=-1.0, scalar2=xdiff[:, I - 1 : I],
             op0=ALU.mult, op1=ALU.min, accum_out=neg_max[:],
         )
+
+        nc.vector.tensor_tensor(
+            out=xdiff[:, slots(1)], in0=ta_sb[:].indirect(list2[:, entries(1)]), in1=slot_b[:, slots(1)],
+            op=ALU.subtract,
+        )
+        nc.vector.tensor_tensor(out=placed1[:].indirect(list1[:]), in0=xdiff[:], in1=share_wide[:], op=ALU.mult)
 
         c0_turned = banks("w")
         cf_turned = sb.tile([P, T], F32)
@@ -226,16 +246,14 @@ def tile_attend_hvborrowed_heads_kernel(
         z = sb.tile([P, 1], F32)
         nc.scalar.activation(out=p[:], in_=neg_s[:], func=ACT.Exp, bias=neg_max[:], scale=-1.0, accum_out=z[:])
 
-        nc.vector.tensor_tensor(out=xs[:], in0=ta_sb[:], in1=placed1[:], op=ALU.add)
+        nc.gpsimd.tensor_tensor(out=xs[:], in0=ta_sb[:], in1=placed1[:], op=ALU.add)
         inv_z = sb.tile([P, 1], F32)
         nc.vector.reciprocal(out=inv_z[:], in_=z[:])
         prob = sb.tile([P, T], F32)
         nc.scalar.activation(out=prob[:], in_=p[:], func=ACT.Copy, scale=inv_z[:])
 
 
-        neg_share_wide = sb.tile([P, I], F32)
-        nc.scalar.activation(out=neg_share_wide[:], in_=share_wide[:], func=ACT.Copy, scale=-1.0)
-        y_turned = banks("z")
+        y_turned = banks("x")
         add_turned(y_turned, base_sb, True, False)
 
         sums = sb.tile([P, 8], F32)
@@ -249,18 +267,18 @@ def tile_attend_hvborrowed_heads_kernel(
                 op0=ALU.mult, op1=ALU.mult, accum_out=sums[:, h : h + 1],
             )
         nc.vector.tensor_scalar(
-            out=sums[:, 2:3], in0=sums[:, 0:1], scalar1=sums[:, 1:2], scalar2=inv_z[:],
+            out=spent[:, 0:1], in0=sums[:, 0:1], scalar1=sums[:, 1:2], scalar2=inv_z[:],
             op0=ALU.add, op1=ALU.mult,
         )
+        for h in range(HALVES):
+            nc.vector.scalar_tensor_tensor(
+                out=pw[:, half(h)], in0=cf_ps[h][:], scalar=spent[:, 0:1], in1=prob[:, half(h)],
+                op0=ALU.subtract, op1=ALU.mult,
+            )
         nc.vector.scalar_tensor_tensor(
             out=spent[:], in0=xs[:], scalar=1.0, in1=prob[:],
             op0=ALU.mult, op1=ALU.mult, accum_out=sums[:, 3:4],
         )
-        for h in range(HALVES):
-            nc.vector.scalar_tensor_tensor(
-                out=pw[:, half(h)], in0=cf_ps[h][:], scalar=sums[:, 2:3], in1=prob[:, half(h)],
-                op0=ALU.subtract, op1=ALU.mult,
-            )
         nc.vector.scalar_tensor_tensor(
             out=t1[:], in0=xs[:], scalar=sums[:, 3:4], in1=pw[:],
             op0=ALU.subtract, op1=ALU.mult, accum_out=sums[:, 4:5],
@@ -271,7 +289,7 @@ def tile_attend_hvborrowed_heads_kernel(
 
         nc.vector.tensor_copy(out=slot_a[:], in_=xds[:].indirect(list1[:]))
         nc.vector.tensor_tensor(out=placed2[:].indirect(list2[:]), in0=slot_a[:], in1=share_wide[:], op=ALU.mult)
-        nc.vector.tensor_tensor(out=placed1[:].indirect(list1[:]), in0=slot_a[:], in1=neg_share_wide[:], op=ALU.mult)
+        nc.vector.tensor_tensor(out=placed1[:].indirect(list1[:]), in0=slot_a[:], in1=share_wide[:], op=ALU.mult)
 
         add_turned(y_turned, xds, False, False)
         add_turned(y_turned, placed2, False, True)
@@ -281,5 +299,5 @@ def tile_attend_hvborrowed_heads_kernel(
         y = sb.tile([P, T], F32)
         for c in range(T // QUARTER):
             cols = slice(c * QUARTER, (c + 1) * QUARTER)
-            nc.vector.tensor_tensor(out=y[:, cols], in0=y_ps[c // 2][:, (c % 2) * QUARTER : (c % 2 + 1) * QUARTER], in1=placed1[:, cols], op=ALU.add)
+            nc.vector.tensor_tensor(out=y[:, cols], in0=y_ps[c // 2][:, (c % 2) * QUARTER : (c % 2 + 1) * QUARTER], in1=placed1[:, cols], op=ALU.subtract)
             nc.sync.dma_start(out=out[:, cols], in_=y[:, cols])

@@ -49,12 +49,6 @@ def tile_attend_hvborrowed_heads_kernel(
         def block(b):
             return slice(b * P, (b + 1) * P)
 
-        def slots(u):
-            return slice(u * I // 2, (u + 1) * I // 2)
-
-        def entries(u):
-            return slice(u * I // 32, (u + 1) * I // 32)
-
         def banks(tag):
             return [ps.tile([P, BANK], F32, name="%s%d" % (tag, h), tag="%s%d" % (tag, h)) for h in range(HALVES)]
 
@@ -167,31 +161,19 @@ def tile_attend_hvborrowed_heads_kernel(
 
         slot_a = sb.tile([P, I], F32)
         slot_b = sb.tile([P, I], F32)
-        for u in range(2):
-            nc.vector.tensor_copy(out=slot_a[:, slots(u)], in_=a_sb[:].indirect(list1[:, entries(u)]))
-        for u in range(2):
-            nc.vector.tensor_tensor(
-                out=slot_b[:, slots(u)], in0=a_sb[:].indirect(list2[:, entries(u)]), in1=slot_a[:, slots(u)],
-                op=ALU.subtract,
-            )
+        nc.vector.tensor_copy(out=slot_a[:], in_=a_sb[:].indirect(list1[:]))
+        nc.vector.tensor_tensor(out=slot_b[:], in0=a_sb[:].indirect(list2[:]), in1=slot_a[:], op=ALU.subtract)
         nc.vector.tensor_tensor(out=placed1[:].indirect(list1[:]), in0=slot_b[:], in1=share_wide[:], op=ALU.mult)
         nc.vector.tensor_copy(out=slot_b[:], in_=ta_sb[:].indirect(list1[:]))
         xdiff = sb.tile([P, I], F32)
-        nc.vector.tensor_tensor(
-            out=xdiff[:, slots(0)], in0=ta_sb[:].indirect(list2[:, entries(0)]), in1=slot_b[:, slots(0)],
-            op=ALU.subtract,
-        )
 
         v_codes = sb.tile([P, T], U32, align_bytes=64)
         v_scales = sb.tile([P, T], U8, align_bytes=64)
-        for h in range(HALVES):
-            v_bf = sb.tile([P, PACK * BANK], BF16, align_bytes=64, name="v_bf%d" % h, tag="v_bf%d" % h)
-            for c in range(BANK // QUARTER):
-                cols = slice(c * PACK * QUARTER, (c + 1) * PACK * QUARTER)
-                interleave(nc.scalar.copy, v_bf[:, cols], v_raw[2 * h + c][:])
-            nc.vector.quantize_mx(
-                out=v_codes[:, half(h)].bitcast(FP8X4), scales=v_scales[:, half(h)], in_=v_bf[:]
-            )
+        v_bf = sb.tile([P, PACK * T], BF16, align_bytes=64, tag="v_bf")
+        for c in range(T // QUARTER):
+            cols = slice(c * PACK * QUARTER, (c + 1) * PACK * QUARTER)
+            interleave(nc.scalar.copy, v_bf[:, cols], v_raw[c][:])
+        nc.vector.quantize_mx(out=v_codes[:].bitcast(FP8X4), scales=v_scales[:], in_=v_bf[:])
 
         g_codes, g_scales = quantised("g", nc.scalar.copy, g_raw)
 
@@ -204,7 +186,7 @@ def tile_attend_hvborrowed_heads_kernel(
 
 
         xs = sb.tile([P, T], F32)
-        neg_s = sb.tile([P, T], F32, align_bytes=64, tag="v_bf1")
+        neg_s = sb.tile([P, T], F32, align_bytes=64, tag="v_bf")
         neg_max = sb.tile([P, 1], F32)
         nc.vector.tensor_scalar(
             out=neg_s[:, half(0)], in0=s_ps[0][:], scalar1=-1.0, scalar2=None,
@@ -215,10 +197,7 @@ def tile_attend_hvborrowed_heads_kernel(
             op0=ALU.mult, op1=ALU.min, accum_out=neg_max[:],
         )
 
-        nc.vector.tensor_tensor(
-            out=xdiff[:, slots(1)], in0=ta_sb[:].indirect(list2[:, entries(1)]), in1=slot_b[:, slots(1)],
-            op=ALU.subtract,
-        )
+        nc.vector.tensor_tensor(out=xdiff[:], in0=ta_sb[:].indirect(list2[:]), in1=slot_b[:], op=ALU.subtract)
         nc.vector.tensor_tensor(out=placed1[:].indirect(list1[:]), in0=xdiff[:], in1=share_wide[:], op=ALU.mult)
 
         c0_turned = banks("w")
@@ -297,7 +276,11 @@ def tile_attend_hvborrowed_heads_kernel(
         turn_back(y_ps, staged, y_turned)
 
         y = sb.tile([P, T], F32)
-        for c in range(T // QUARTER):
+        y_first = sb.tile([P, QUARTER], F32)
+        nc.scalar.copy(out=y_first[:], in_=y_ps[0][:, 0:QUARTER])
+        nc.gpsimd.tensor_tensor(out=y[:, 0:QUARTER], in0=y_first[:], in1=placed1[:, 0:QUARTER], op=ALU.subtract)
+        nc.scalar.dma_start(out=out[:, 0:QUARTER], in_=y[:, 0:QUARTER])
+        for c in range(1, T // QUARTER):
             cols = slice(c * QUARTER, (c + 1) * QUARTER)
             nc.vector.tensor_tensor(out=y[:, cols], in0=y_ps[c // 2][:, (c % 2) * QUARTER : (c % 2 + 1) * QUARTER], in1=placed1[:, cols], op=ALU.subtract)
             nc.sync.dma_start(out=out[:, cols], in_=y[:, cols])

from contextlib import ExitStack

import concourse.mybir as mybir
from concourse.masks import make_identity

D, E, T, Q, I = 512, 512, 1024, 128, 512
FLOPS = 2 * Q * T * (2 * D + E)

F32 = mybir.dt.float32
BF16 = mybir.dt.bfloat16
I32 = mybir.dt.int32
U32 = mybir.dt.uint32
U16 = mybir.dt.uint16
U8 = mybir.dt.uint8
FP8X4 = mybir.dt.float8_e4m3fn_x4
FP4X4 = mybir.dt.float4_e2m1fn_x4
ALU = mybir.AluOpType
ACT = mybir.ActivationFunctionType

P = 128
PACK = 4
BANK = 512
HALVES = T // BANK
BLOCKS = T // P
PER_BANK = BANK // P
QUARTER = 256
OUT_FACTOR = 1024.0


def interleave(copy, grouped, raw):
    copy(
        out=grouped.rearrange("p (c i t) -> p c t i", i=4, t=PACK),
        in_=raw.rearrange("p t (c i) -> p c t i", i=4),
    )


def tile_attend_hvborrowed_heads_kernel(
    tc, query, keys_words, keys_scales, gout, vals, share, fac, dquery, base, offs, offs2, out
):
    nc = tc.nc
    with ExitStack() as ctx:
        lists = ctx.enter_context(tc.tile_pool(name="lists", bufs=1))
        sb = ctx.enter_context(tc.tile_pool(name="sb", bufs=1))
        ps = ctx.enter_context(tc.psum_pool(name="ps", bufs=1))

        def half(h):
            return slice(h * BANK, (h + 1) * BANK)

        def block(b):
            return slice(b * P, (b + 1) * P)

        def banks(tag):
            return [ps.tile([P, BANK], F32, name="%s%d" % (tag, h), tag="%s%d" % (tag, h)) for h in range(HALVES)]

        def bank_block(pair, b):
            return pair[b // PER_BANK][:, block(b % PER_BANK)]

        k_scales = sb.tile([P, T], U8, align_bytes=64)
        nc.vector.memset(k_scales[:].bitcast(U32), 0)

        q_raw = sb.tile([P, PACK, Q], F32)
        nc.sync.dma_start(out=q_raw[:], in_=query.rearrange("(p t) w -> p t w", t=PACK))
        k_words = sb.tile([P, 2 * T], U8, align_bytes=64)
        nc.sync.dma_start(out=k_words[:].bitcast(I32), in_=keys_words[0].bitcast(I32))
        for quad in range(4):
            nc.sync.dma_start(
                out=k_scales[32 * quad : 32 * quad + 4, :].bitcast(I32),
                in_=keys_scales[0, 4 * quad : 4 * quad + 4, :].bitcast(I32),
            )
        dq_raw = sb.tile([P, PACK, Q], F32)
        nc.sync.dma_start(out=dq_raw[:], in_=dquery.rearrange("(p t) w -> p t w", t=PACK))
        list1 = lists.tile([P, I // 16], U16)
        nc.sync.dma_start(list1[:], offs)
        list2 = lists.tile([P, I // 16], U16)
        nc.sync.dma_start(list2[:], offs2)
        share_col = sb.tile([P, 1], F32)
        nc.sync.dma_start(out=share_col[:], in_=share)
        fac_rows = sb.tile([P, P], F32)
        nc.gpsimd.memset(fac_rows[:], 0.0)
        nc.sync.dma_start(out=fac_rows[0:BLOCKS, :], in_=fac.rearrange("o (c p) -> (o c) p", p=P))
        v_raw = []
        for c in range(T // QUARTER):
            chunk = sb.tile([P, PACK, QUARTER], F32, name="v_raw%d" % c, tag="v_raw%d" % c)
            nc.sync.dma_start(
                out=chunk[:],
                in_=vals[:, c * QUARTER : (c + 1) * QUARTER].rearrange("(p t) w -> p t w", t=PACK),
            )
            v_raw.append(chunk)
        g_raw = sb.tile([P, PACK, Q], F32)
        nc.sync.dma_start(out=g_raw[:], in_=gout.rearrange("(p t) w -> p t w", t=PACK))
        base_sb = sb.tile([P, T], F32)
        nc.sync.dma_start(out=base_sb[:], in_=base)

        ident = sb.tile([P, P], F32)
        make_identity(nc, ident[:])

        placed1 = sb.tile([P, T], F32)
        placed2 = sb.tile([P, T], F32)
        nc.vector.memset(placed1[:], 0.0)
        nc.vector.memset(placed2[:], 0.0)

        def quantised(name, copy, raw):
            grouped = sb.tile([P, PACK * Q], BF16, align_bytes=64, name=name + "_bf")
            codes = sb.tile([P, Q], U32, align_bytes=64, name=name + "_codes")
            scales = sb.tile([P, Q], U8, align_bytes=64, name=name + "_scales")
            interleave(copy, grouped[:], raw[:])
            nc.vector.quantize_mx(out=codes[:].bitcast(FP8X4), scales=scales[:], in_=grouped[:])
            return codes, scales

        def against_keys(acc, codes, scales, col0, width):
            nc.tensor.matmul_mx(
                out=acc,
                lhsT=codes[:].bitcast(FP8X4),
                lhsT_scale=scales[:],
                rhs=k_words[:, 2 * col0 : 2 * (col0 + width)].bitcast(FP4X4),
                rhs_scale=k_scales[:, col0 : col0 + width],
                start=True,
                stop=True,
            )

        def add_turned(acc, src, first, last):
            for b in range(BLOCKS):
                nc.tensor.matmul(
                    out=bank_block(acc, b),
                    lhsT=src[:, block(b)],
                    rhs=ident[:],
                    start=first and b % PER_BANK == 0,
                    stop=last and b % PER_BANK == PER_BANK - 1,
                    is_transpose=True,
                )

        def turn_back(acc_back, staged, acc):
            for h in range(HALVES):
                nc.scalar.copy(out=staged[:, half(h)], in_=acc[h][:])
            for b in range(BLOCKS):
                nc.tensor.transpose(bank_block(acc_back, b), staged[:, block(b)], ident[:])

        q_codes, q_scales = quantised("q", nc.vector.tensor_copy, q_raw)
        a_ps = banks("w") + banks("x")
        a_sb = sb.tile([P, T], F32)
        for c in range(T // QUARTER):
            acc = a_ps[c][:, 0:QUARTER]
            against_keys(acc, q_codes, q_scales, c * QUARTER, QUARTER)
            copy = (nc.scalar.copy, nc.vector.tensor_copy)[c % 2]
            copy(out=a_sb[:, c * QUARTER : (c + 1) * QUARTER], in_=acc)

        dq_codes, dq_scales = quantised("dq", nc.vector.tensor_copy, dq_raw)
        ta_ps = banks("y")
        ta_sb = sb.tile([P, T], F32)
        for h in range(HALVES):
            against_keys(ta_ps[h][:], dq_codes, dq_scales, h * BANK, BANK)
            nc.scalar.copy(out=ta_sb[:, half(h)], in_=ta_ps[h][:])

        share_wide = sb.tile([P, I], F32)
        nc.scalar.activation(out=share_wide[:], in_=share_col[:].to_broadcast([P, I]), func=ACT.Copy)

        fac_ps = ps.tile([P, BANK], F32, tag="z0")
        nc.tensor.transpose(fac_ps[:, 0:P], fac_rows[:], ident[:])
        fac_cols = sb.tile([P, BLOCKS], F32)
        nc.scalar.activation(out=fac_cols[:], in_=fac_ps[:, 0:BLOCKS], func=ACT.Copy, scale=-OUT_FACTOR)

        slot_a = sb.tile([P, I], F32)
        slot_b = sb.tile([P, I], F32)
        nc.vector.tensor_copy(out=slot_a[:], in_=a_sb[:].indirect(list1[:]))
        nc.vector.tensor_tensor(out=slot_b[:], in0=a_sb[:].indirect(list2[:]), in1=slot_a[:], op=ALU.subtract)
        nc.vector.tensor_tensor(out=placed1[:].indirect(list1[:]), in0=slot_b[:], in1=share_wide[:], op=ALU.mult)
        nc.vector.tensor_copy(out=slot_b[:], in_=ta_sb[:].indirect(list1[:]))
        xdiff = sb.tile([P, I], F32)

        v_codes = sb.tile([P, T], U32, align_bytes=64)
        v_scales = sb.tile([P, T], U8, align_bytes=64)
        v_bf = sb.tile([P, PACK * T], BF16, align_bytes=64, tag="v_bf")
        for c in range(T // QUARTER):
            cols = slice(c * PACK * QUARTER, (c + 1) * PACK * QUARTER)
            interleave(nc.scalar.copy, v_bf[:, cols], v_raw[c][:])
        nc.vector.quantize_mx(out=v_codes[:].bitcast(FP8X4), scales=v_scales[:], in_=v_bf[:])

        g_codes, g_scales = quantised("g", nc.scalar.copy, g_raw)

        s_turned = banks("w")
        add_turned(s_turned, a_sb, True, False)
        add_turned(s_turned, placed1, False, True)
        staged = sb.tile([P, T], F32, tag="v_raw3")
        s_ps = banks("x")
        turn_back(s_ps, staged, s_turned)


        xs = sb.tile([P, T], F32)
        neg_s = sb.tile([P, T], F32, align_bytes=64, tag="v_bf")
        neg_max = sb.tile([P, 1], F32)
        nc.vector.tensor_scalar(
            out=neg_s[:, half(0)], in0=s_ps[0][:], scalar1=-1.0, scalar2=None,
            op0=ALU.mult, op1=ALU.min, accum_out=xdiff[:, I - 1 : I],
        )
        nc.vector.tensor_scalar(
            out=neg_s[:, half(1)], in0=s_ps[1][:], scalar1=-1.0, scalar2=xdiff[:, I - 1 : I],
            op0=ALU.mult, op1=ALU.min, accum_out=neg_max[:],
        )

        nc.vector.tensor_tensor(out=xdiff[:], in0=ta_sb[:].indirect(list2[:]), in1=slot_b[:], op=ALU.subtract)
        nc.vector.tensor_tensor(out=placed1[:].indirect(list1[:]), in0=xdiff[:], in1=share_wide[:], op=ALU.mult)

        c0_turned = banks("w")
        cf_turned = sb.tile([P, T], F32)
        cf_ps = banks("y")
        for b in range(BLOCKS):
            nc.tensor.matmul_mx(
                out=bank_block(c0_turned, b),
                lhsT=v_codes[:, block(b)].bitcast(FP8X4),
                lhsT_scale=v_scales[:, block(b)],
                rhs=g_codes[:].bitcast(FP8X4),
                rhs_scale=g_scales[:],
                start=True,
                stop=True,
            )
        for b in range(BLOCKS):
            nc.scalar.activation(
                out=cf_turned[:, block(b)], in_=bank_block(c0_turned, b), func=ACT.Copy,
                scale=fac_cols[:, b : b + 1],
            )
        for b in range(BLOCKS):
            nc.tensor.transpose(bank_block(cf_ps, b), cf_turned[:, block(b)], ident[:])

        p = sb.tile([P, T], F32)
        z = sb.tile([P, 1], F32)
        nc.scalar.activation(out=p[:], in_=neg_s[:], func=ACT.Exp, bias=neg_max[:], scale=-1.0, accum_out=z[:])

        nc.gpsimd.tensor_tensor(out=xs[:], in0=ta_sb[:], in1=placed1[:], op=ALU.add)
        inv_z = sb.tile([P, 1], F32)
        nc.vector.reciprocal(out=inv_z[:], in_=z[:])
        prob = sb.tile([P, T], F32)
        nc.scalar.activation(out=prob[:], in_=p[:], func=ACT.Copy, scale=inv_z[:])


        y_turned = banks("x")
        add_turned(y_turned, base_sb, True, False)

        sums = sb.tile([P, 8], F32)
        spent = sb.tile([P, T], F32)
        pw = sb.tile([P, T], F32)
        t1 = sb.tile([P, T], F32)
        xds = sb.tile([P, T], F32)
        for h in range(HALVES):
            nc.vector.scalar_tensor_tensor(
                out=spent[:, half(h)], in0=cf_ps[h][:], scalar=1.0, in1=p[:, half(h)],
                op0=ALU.mult, op1=ALU.mult, accum_out=sums[:, h : h + 1],
            )
        nc.vector.tensor_scalar(
            out=spent[:, 0:1], in0=sums[:, 0:1], scalar1=sums[:, 1:2], scalar2=inv_z[:],
            op0=ALU.add, op1=ALU.mult,
        )
        for h in range(HALVES):
            nc.vector.scalar_tensor_tensor(
                out=pw[:, half(h)], in0=cf_ps[h][:], scalar=spent[:, 0:1], in1=prob[:, half(h)],
                op0=ALU.subtract, op1=ALU.mult,
            )
        nc.vector.scalar_tensor_tensor(
            out=spent[:], in0=xs[:], scalar=1.0, in1=prob[:],
            op0=ALU.mult, op1=ALU.mult, accum_out=sums[:, 3:4],
        )
        nc.vector.scalar_tensor_tensor(
            out=t1[:], in0=xs[:], scalar=sums[:, 3:4], in1=pw[:],
            op0=ALU.subtract, op1=ALU.mult, accum_out=sums[:, 4:5],
        )
        nc.vector.scalar_tensor_tensor(
            out=xds[:], in0=prob[:], scalar=sums[:, 4:5], in1=t1[:], op0=ALU.mult, op1=ALU.subtract
        )

        nc.vector.tensor_copy(out=slot_a[:], in_=xds[:].indirect(list1[:]))
        nc.vector.tensor_tensor(out=placed2[:].indirect(list2[:]), in0=slot_a[:], in1=share_wide[:], op=ALU.mult)
        nc.vector.tensor_tensor(out=placed1[:].indirect(list1[:]), in0=slot_a[:], in1=share_wide[:], op=ALU.mult)

        add_turned(y_turned, xds, False, False)
        add_turned(y_turned, placed2, False, True)
        y_ps = banks("w")
        turn_back(y_ps, staged, y_turned)

        y = sb.tile([P, T], F32)
        y_first = sb.tile([P, QUARTER], F32)
        nc.scalar.copy(out=y_first[:], in_=y_ps[0][:, 0:QUARTER])
        nc.gpsimd.tensor_tensor(out=y[:, 0:QUARTER], in0=y_first[:], in1=placed1[:, 0:QUARTER], op=ALU.subtract)
        nc.scalar.dma_start(out=out[:, 0:QUARTER], in_=y[:, 0:QUARTER])
        for c in range(1, T // QUARTER):
            cols = slice(c * QUARTER, (c + 1) * QUARTER)
            nc.vector.tensor_tensor(out=y[:, cols], in0=y_ps[c // 2][:, (c % 2) * QUARTER : (c % 2 + 1) * QUARTER], in1=placed1[:, cols], op=ALU.subtract)
            nc.sync.dma_start(out=out[:, cols], in_=y[:, cols])
